import numpy as np
import ml_dtypes


def mxq(x, axis, fmt="e4m3"):
    dtype, down = {"e4m3": (ml_dtypes.float8_e4m3fn, 7), "e5m2": (ml_dtypes.float8_e5m2, 14)}[fmt]
    v = np.moveaxis(np.asarray(x, np.float32).astype(ml_dtypes.bfloat16).astype(np.float64), axis, -1)
    blocks = v.reshape(v.shape[:-1] + (-1, 32))
    amax = np.abs(blocks).max(-1, keepdims=True)
    byte = np.maximum(np.where(amax > 0, np.frexp(amax)[1] - 1 + 127, 0) - down, 1)
    scale = np.exp2(byte - 127.0)
    codes = (blocks / scale).astype(np.float32).astype(dtype).astype(np.float64)
    return np.moveaxis((codes * scale).reshape(v.shape), -1, axis)


WIDE = False


def mx_kscale(k):
    if not WIDE:
        return np.ones(k)
    levels = np.array([10, -10, 5, -5, 0])
    if k % 512:
        return np.exp2(np.random.permutation(np.resize(levels, k // 32))).repeat(32)
    a = np.empty((k // 512, 16))
    for p in range(k // 512):
        a[p, :8] = np.random.permutation(np.resize(levels, 8))
        for g in range(8):
            far = levels[np.abs(levels - a[p, g]) >= 10]
            a[p, g + 8] = far[np.random.randint(len(far))]
    return np.exp2(a.ravel()).repeat(32)


def f64(x):
    return np.asarray(x).astype(np.float64)


def striped(idx):
    return np.tile(idx.reshape(-1, 16).T, (8, 1)).astype(np.uint16)


def unstriped(offs):
    return offs[:16].T.reshape(-1).astype(np.int64)


E2M1 = np.array([0.0, 0.5, 1.0, 1.5, 2.0, 3.0, 4.0, 6.0, -0.0, -0.5, -1.0, -1.5, -2.0, -3.0, -4.0, -6.0])


def pack_weight(w, fmt):
    k, n = w.shape
    w = f64(np.asarray(w, np.float32).astype(ml_dtypes.bfloat16)).reshape(k // 32, 32, n)
    amax = np.abs(w).max(1)
    if fmt == "e4m3":
        byte = np.frexp(amax)[1] - 1 + 127 - 7
    else:
        mant, ex = np.frexp(amax / 6.0)
        byte = np.where(mant > 0.5, ex, ex - 1) + 127
    byte = np.clip(np.where(amax > 0, byte, 1), 1, 254)
    scaled = (w * np.exp2(127.0 - byte)[:, None, :]).reshape(k, n).astype(np.float32)
    by_word = np.ascontiguousarray(scaled.reshape(k // 512, 128, 4, n).transpose(0, 1, 3, 2))
    if fmt == "e4m3":
        words = by_word.astype(ml_dtypes.float8_e4m3fn).view(np.uint8)
    else:
        c = by_word.astype(ml_dtypes.float4_e2m1fn).view(np.uint8) & 0xF
        words = (c[..., 0::2] | (c[..., 1::2] << 4)).reshape(k // 512, 128, 2 * n)
    return np.ascontiguousarray(words), np.ascontiguousarray(byte.astype(np.uint8).reshape(k // 512, 16, n))


def unpack_weight(words, scales, fmt):
    g, _, n = scales.shape
    words = np.ascontiguousarray(words).reshape(g, 128, n, -1)
    if fmt == "e4m3":
        vals = words.view(ml_dtypes.float8_e4m3fn).astype(np.float64)
    else:
        nib = np.empty((g, 128, n, 4), np.uint8)
        nib[..., 0::2] = words & 0xF
        nib[..., 1::2] = words >> 4
        vals = E2M1[nib]
    vals = vals * np.repeat(np.exp2(scales.astype(np.float64) - 127.0), 8, axis=1)[..., None]
    return vals.transpose(0, 1, 3, 2).reshape(g * 512, n)


def gelu(v):
    return 0.5 * v * (1.0 + np.tanh(np.sqrt(2.0 / np.pi) * (v + 0.044715 * v**3)))


K, H, T, S, T2, P, Q = 1536, 1024, 2048, 512, 1024, 512, 128

def setup_inputs():
    n = np.random.standard_normal
    s = mx_kscale(K)[:, None]
    u = mx_kscale(H)[:, None]
    d = {}
    d["tab_words"], d["tab_scales"] = pack_weight(n((K, T)) * s, "e4m3")
    d["offs"] = striped(np.random.permutation(T)[:S])
    d["offs2"] = striped(np.random.permutation(T2)[:S])
    d["offs3"] = striped(np.random.permutation(T2)[:P])
    d["w1"] = (1.6 * n((K, H)) / K**0.5 / s).astype(np.float32)
    d["w4_words"], d["w4_scales"] = pack_weight(1.6 * n((K, H)) / K**0.5 / s, "e2m1")
    d["gain"] = (0.6 * np.exp(0.3 * n(H)) * u[:, 0]).astype(np.float32)
    d["wgs"] = np.exp(0.3 * n((Q, S))).astype(np.float32)
    d["page0"] = (n((H, T2)) * u).astype(np.float32)
    d["sq"] = (0.5 * np.exp(0.5 * n(H)) * u[:, 0]**2).astype(np.float32)
    d["gv"] = (0.7 * n(H) / H**0.5 / u[:, 0]**2).astype(np.float32)
    d["base"] = (0.7 * n((T2, P))).astype(np.float32)
    return d

def reference(tab_words, tab_scales, offs, offs2, offs3, w1, w4_words, w4_scales, gain, wgs, page0, sq, gv, base):
    v = unpack_weight(tab_words, tab_scales, "e4m3")[:, unstriped(offs)]
    a = mxq(f64(w1), 0, "e4m3").T @ v
    b = unpack_weight(w4_words, w4_scales, "e2m1").T @ v
    h = (np.tanh(a) * b + a) * f64(gain)[:, None]
    page = f64(page0).copy()
    page[:, unstriped(offs2)] = np.tile(f64(wgs), (H // Q, 1)) * h
    x = np.sqrt(np.square(page[:, unstriped(offs3)]) + f64(sq)[:, None]) * f64(gv)[:, None]
    e = mxq(page, 0, "e4m3").T @ mxq(x, 0, "e4m3")
    return np.tanh(e + f64(base))

@@ -1,0 +1,351 @@
+from contextlib import ExitStack
+
+import concourse.mybir as mybir
+from concourse.masks import make_identity
+
+K, H, T, S, T2, NB = 1536, 1024, 2048, 512, 1024, 512
+FLOPS = 2 * (2 * K * H * S + H * T2 * NB)
+
+F32 = mybir.dt.float32
+BF16 = mybir.dt.bfloat16
+I32 = mybir.dt.int32
+U32 = mybir.dt.uint32
+U16 = mybir.dt.uint16
+U8 = mybir.dt.uint8
+FP8X4 = mybir.dt.float8_e4m3fn_x4
+FP4X4 = mybir.dt.float4_e2m1fn_x4
+MULT = mybir.AluOpType.mult
+ADD = mybir.AluOpType.add
+ACT = mybir.ActivationFunctionType
+
+P = 128
+PACK = 4
+KP = P * PACK
+KA = K // KP
+RB = H // KP
+AL = 64
+
+
+def tile_list_bogie_benchmark_scores_kernel(
+    tc, tab_words, tab_scales, offs, offs2, offs3, w1, w4_words, w4_scales, gain, wgs, page0, sq, gv, base, out
+):
+    nc = tc.nc
+    with ExitStack() as ctx:
+        keep = ctx.enter_context(tc.tile_pool(name="keep", bufs=1))
+        ring = ctx.enter_context(tc.tile_pool(name="ring", bufs=4))
+        psum = ctx.enter_context(tc.psum_pool(name="psum", bufs=1))
+
+        def sb(shape, dtype, name, tag=None):
+            return keep.tile(shape, dtype, name=name, tag=tag or name, align_bytes=AL)
+
+        def bank(i, name):
+            return psum.tile([P, 512], F32, name=name, tag="bank%d" % i)
+
+        tab_sc = sb([P, KA, T], U8, "tab_sc")
+        w4_sc_raw = sb([P, KA, H], U8, "w4_sc_raw", "xin1")
+        rows = sb([P, 2 * P], F32, "rows")
+        zero = sb([P, 1], F32, "zero")
+        ident = sb([P, P], F32, "ident")
+        nc.vector.memset(tab_sc[:].rearrange("p a t -> p (a t)").bitcast(I32), 0)
+        nc.vector.memset(w4_sc_raw[:].rearrange("p a c -> p (a c)").bitcast(I32), 0)
+        nc.vector.memset(rows[:], 0.0)
+        nc.vector.memset(zero[:], 0.0)
+        zero_bias = sb([P, 1], F32, "zero_bias", "root")
+        nc.scalar.activation(zero_bias[:], zero[:], ACT.Tanh)
+
+        idx1 = sb([P, S // 16], U16, "idx1")
+        idx2 = sb([P, S // 16], U16, "idx2")
+        idx3 = sb([P, NB // 16], U16, "idx3")
+        nc.sync.dma_start(idx1[:], offs)
+        for q in range(4):
+            nc.gpsimd.dma_start(
+                tab_sc[32 * q : 32 * q + 4, :, :].bitcast(I32),
+                tab_scales[:, 4 * q : 4 * q + 4, :].rearrange("a r t -> r a t").bitcast(I32),
+            )
+        for q in range(4):
+            nc.gpsimd.dma_start(
+                w4_sc_raw[32 * q : 32 * q + 4, :, :].bitcast(I32),
+                w4_scales[:, 4 * q : 4 * q + 4, :].rearrange("a r c -> r a c").bitcast(I32),
+            )
+        for v, vec in enumerate((gain, sq, gv)):
+            nc.gpsimd.dma_start(
+                rows[4 * v : 4 * v + 4, :].rearrange("t (n i) -> t n i", i=4),
+                vec.rearrange("(n t i) -> t n i", t=4, i=4),
+            )
+
+        make_identity(nc, ident[:])
+
+        stage_tags = ["stage0", "stage1", "stage2"]
+        w1_raw = {}
+        tab = {}
+        w4_raw = {}
+        page = {}
+        wg = {}
+
+        def load_w1(b, a):
+            w1_raw[b, a] = sb([P, PACK, KP], F32, "w1_raw%d%d" % (b, a), stage_tags[a])
+            nc.sync.dma_start(
+                w1_raw[b, a][:], w1[KP * a : KP * (a + 1), KP * b : KP * (b + 1)].rearrange("(p j) c -> p j c", j=PACK)
+            )
+
+        def load_tab(a):
+            tab[a] = sb([P, T], U32, "tab%d" % a)
+            nc.sync.dma_start(tab[a][:].bitcast(I32), tab_words[a].rearrange("p t i -> p (t i)").bitcast(I32))
+
+        def load_w4(b):
+            w4_raw[b] = sb([P, KA, 2 * KP], U8, "w4_raw%d" % b, "pin1" if b == 1 else None)
+            nc.sync.dma_start(
+                w4_raw[b][:].bitcast(I32),
+                w4_words.rearrange("a p c -> p a c")[:, :, 2 * KP * b : 2 * KP * (b + 1)].bitcast(I32),
+            )
+
+        def load_page(s):
+            b, t = divmod(s, PACK)
+            page[s] = sb([P, T2], F32, "page%d" % s)
+            nc.sync.dma_start(
+                page[s][:], page0[KP * b : KP * (b + 1), :].rearrange("(n t i) m -> t n i m", t=4, i=4)[t]
+            )
+
+        def load_wg(t):
+            wg[t] = sb([P, S], F32, "wg%d" % t)
+            for c in range(4):
+                (nc.gpsimd if t == 0 else nc.sync).dma_start(wg[t][32 * c : 32 * c + 32, :], wgs.rearrange("(n t i) j -> t n i j", t=4, i=4)[t])
+
+        w1_in = {}
+        w1_q = {}
+        w1_s = {}
+
+        def cast_w1(b, a, split):
+            tag = "held" if (b, a) == (1, 2) else "w1_in%d" % (a % 2)
+            w1_in[b, a] = sb([P, PACK * KP], BF16, "w1_in%d%d" % (b, a), tag)
+            dst = w1_in[b, a][:].rearrange("p (t n i j) -> p t n j i", t=4, i=4, j=4)
+            src = w1_raw[b, a][:].rearrange("p j (n t i) -> p t n j i", t=4, i=4)
+            if split:
+                nc.vector.tensor_copy(dst[:, 0:2], src[:, 0:2])
+                nc.scalar.copy(dst[:, 2:4], src[:, 2:4])
+            else:
+                nc.scalar.copy(dst, src)
+
+        def quant_w1(b, a):
+            w1_q[b, a] = sb([P, KP], U32, "w1_q%d%d" % (b, a))
+            w1_s[b, a] = sb([P, KP], U8, "w1_s%d%d" % (b, a))
+            nc.vector.quantize_mx(w1_q[b, a][:].bitcast(FP8X4), w1_s[b, a][:], w1_in[b, a][:])
+
+        w4_q = {}
+
+        def deal_w4(b):
+            w4_q[b] = sb([P, KA, 2 * KP], U8, "w4_q%d" % b)
+            nc.vector.tensor_copy(
+                w4_q[b][:].bitcast(I32).rearrange("p a (t n w) -> p a t n w", t=4, w=2),
+                w4_raw[b][:].bitcast(I32).rearrange("p a (n t w) -> p a t n w", t=4, w=2),
+            )
+
+        load_w1(0, 0)
+        load_tab(0)
+        load_w4(0)
+        load_w1(0, 1)
+        load_tab(1)
+        load_w1(0, 2)
+        load_tab(2)
+        nc.sync.dma_start(idx2[:], offs2)
+        load_wg(0)
+        load_page(0)
+        nc.sync.dma_start(idx3[:], offs3)
+        load_page(1)
+        load_wg(1)
+
+        vecs = sb([P, RB, 12], F32, "vecs")
+        turned = bank(7, "turned")
+        for b in range(RB):
+            nc.tensor.transpose(turned[:, P * b : P * (b + 1)], rows[:, P * b : P * (b + 1)], ident[:])
+        nc.scalar.copy(vecs[:], turned[:, 0 : 2 * P].rearrange("p (b c) -> p b c", b=RB)[:, :, 0:12])
+
+        def vec_col(v, s):
+            b, t = divmod(s, PACK)
+            return vecs[:, b, 4 * v + t : 4 * v + t + 1]
+
+        v_s = sb([P, KA, S], U8, "v_s")
+        for a in range(KA):
+            nc.vector.tensor_copy(v_s[:, a, :], tab_sc[:, a, :].indirect(idx1[:]))
+        w4_s = sb([P, KA, H], U8, "w4_s")
+        nc.vector.tensor_copy(
+            w4_s[:].bitcast(I32).rearrange("p a (b t n) -> p a b t n", b=RB, t=4),
+            w4_sc_raw[:].bitcast(I32).rearrange("p a (b n t) -> p a b t n", b=RB, t=4),
+        )
+        v_q = {}
+        for a in range(KA):
+            cast_w1(0, a, a == KA - 1)
+            quant_w1(0, a)
+            v_q[a] = sb([P, S], U32, "v_q%d" % a)
+            nc.vector.tensor_copy(v_q[a][:], tab[a][:].indirect(idx1[:]))
+            if a == 0:
+                deal_w4(0)
+
+        acc_a = {}
+        acc_b = {}
+
+        def first_products(b):
+            for t in range(PACK):
+                acc_a[PACK * b + t] = bank(2 * t, "acc_a%d%d" % (b, t))
+                acc_b[PACK * b + t] = bank(2 * t + 1, "acc_b%d%d" % (b, t))
+            for a in range(KA):
+                for t in range(PACK):
+                    s = PACK * b + t
+                    nc.tensor.matmul_mx(
+                        acc_a[s][:],
+                        lhsT=w1_q[b, a][:, P * t : P * (t + 1)].bitcast(FP8X4),
+                        lhsT_scale=w1_s[b, a][:, P * t : P * (t + 1)],
+                        rhs=v_q[a][:].bitcast(FP8X4),
+                        rhs_scale=v_s[:, a, :],
+                        start=(a == 0),
+                        stop=(a == KA - 1),
+                    )
+                    nc.tensor.matmul_mx(
+                        acc_b[s][:],
+                        lhsT=w4_q[b][:, a, 2 * P * t : 2 * P * (t + 1)].bitcast(FP4X4),
+                        lhsT_scale=w4_s[:, a, KP * b + P * t : KP * b + P * (t + 1)],
+                        rhs=v_q[a][:].bitcast(FP8X4),
+                        rhs_scale=v_s[:, a, :],
+                        start=(a == 0),
+                        stop=(a == KA - 1),
+                    )
+
+        th = {}
+
+        def tanh_a(b):
+            for t in range(PACK):
+                s = PACK * b + t
+                th[s] = ring.tile([P, S], F32, name="th%d" % s, tag="th")
+                nc.scalar.activation(th[s][:], acc_a[s][:], ACT.Tanh, bias=zero_bias[:])
+
+        first_products(0)
+        tanh_a(0)
+
+        load_w1(1, 0)
+        load_w4(1)
+        load_page(2)
+        load_wg(2)
+        load_w1(1, 1)
+        load_page(3)
+        load_wg(3)
+        load_w1(1, 2)
+        for s in range(4, 8):
+            load_page(s)
+        deal_w4(1)
+        for a in range(KA):
+            cast_w1(1, a, False)
+            quant_w1(1, a)
+
+        picked = {}
+        pairs = {}
+        held_u = {7: "pin0"}
+        held_h = {3: "held", 7: "xin0"}
+
+        def features(s):
+            if s in held_u:
+                u = sb([P, S], F32, "u%d" % s, held_u[s])
+            else:
+                u = ring.tile([P, S], F32, name="u%d" % s, tag="u", bufs=2)
+            if s in held_h:
+                h = sb([P, S], F32, "h%d" % s, held_h[s])
+            else:
+                h = ring.tile([P, S], F32, name="h%d" % s, tag="h", bufs=3)
+            nc.vector.scalar_tensor_tensor(u[:], acc_b[s][:], vec_col(0, s), th[s][:], MULT, MULT)
+            nc.vector.scalar_tensor_tensor(h[:], acc_a[s][:], vec_col(0, s), u[:], MULT, ADD)
+            return h
+
+        def place(s, h):
+            b, t = divmod(s, PACK)
+            nc.vector.tensor_tensor(page[s][:].indirect(idx2[:]), h[:], wg[t][:], MULT)
+            if t == 0:
+                pairs[b] = sb([P, 2, T2, 2], BF16, "pairs%d" % b, stage_tags[b])
+            nc.gpsimd.tensor_scalar(pairs[b][:, t // 2, :, t % 2], page[s][:], 1.0, 0.0, MULT, ADD)
+
+        def pick(s):
+            picked[s] = ring.tile([P, NB], F32, name="picked%d" % s, tag="picked")
+            nc.vector.tensor_copy(picked[s][:], page[s][:].indirect(idx3[:]))
+
+        root = {}
+        xpairs = {}
+
+        def magnitudes(b, ts):
+            if b not in root:
+                root[b] = sb([P, PACK, NB], F32, "root%d" % b, "root")
+                xpairs[b] = sb([P, 2, NB, 2], BF16, "xpairs%d" % b, "xpairs")
+            for t in ts:
+                nc.scalar.activation(root[b][:, t, :], picked[PACK * b + t][:], ACT.Square)
+            for t in ts:
+                nc.scalar.activation(root[b][:, t, :], root[b][:, t, :], ACT.Sqrt, bias=vec_col(1, PACK * b + t))
+            for t in ts:
+                nc.scalar.activation(
+                    xpairs[b][:, t // 2, :, t % 2], root[b][:, t, :], ACT.Copy, scale=vec_col(2, PACK * b + t)
+                )
+
+        p_q, p_s, x_q, x_s = {}, {}, {}, {}
+
+        def weave(copy, src, width, name, tag):
+            woven = sb([P, width, 2], F32, name, tag)
+            copy(woven[:], src[:].rearrange("p u c e -> p u (c e)").bitcast(F32).rearrange("p u c -> p c u"))
+            return woven[:].rearrange("p c u -> p (c u)").bitcast(BF16)
+
+        def quant_pass(b, copy):
+            p_in = weave(copy, pairs[b], T2, "p_in%d" % b, "pin%d" % b)
+            x_in = weave(copy, xpairs[b], NB, "x_in%d" % b, "xin%d" % b)
+            p_q[b] = sb([P, T2], U32, "p_q%d" % b)
+            p_s[b] = sb([P, T2], U8, "p_s%d" % b)
+            x_q[b] = sb([P, NB], U32, "x_q%d" % b)
+            x_s[b] = sb([P, NB], U8, "x_s%d" % b)
+            nc.vector.quantize_mx(p_q[b][:].bitcast(FP8X4), p_s[b][:], p_in)
+            nc.vector.quantize_mx(x_q[b][:].bitcast(FP8X4), x_s[b][:], x_in)
+
+        score = {}
+
+        def second_product(b, n):
+            if b == 0:
+                score[n] = bank(n, "score%d" % n)
+            nc.tensor.matmul_mx(
+                score[n][:],
+                lhsT=p_q[b][:, P * n : P * (n + 1)].bitcast(FP8X4),
+                lhsT_scale=p_s[b][:, P * n : P * (n + 1)],
+                rhs=x_q[b][:].bitcast(FP8X4),
+                rhs_scale=x_s[b][:],
+                start=(b == 0),
+                stop=(b == RB - 1),
+            )
+
+        for s in range(0, 4):
+            h = features(s)
+            if s > 0:
+                pick(s - 1)
+            place(s, h)
+        first_products(1)
+        tanh_a(1)
+        h = features(4)
+        pick(3)
+        place(4, h)
+        magnitudes(0, range(PACK))
+        quant_pass(0, nc.scalar.copy)
+
+        offset = {}
+        for half, tag in ((0, stage_tags[2]), (1, stage_tags[0])):
+            offset[half] = sb([P, 4, NB], F32, "offset%d" % half, tag)
+            nc.sync.dma_start(
+                offset[half][:], base[KP * half : KP * (half + 1), :].rearrange("(n p) j -> p n j", p=P)
+            )
+
+        for s in range(5, 8):
+            h = features(s)
+            pick(s - 1)
+            place(s, h)
+            magnitudes(1, [s - 5])
+        for n in range(T2 // P):
+            second_product(0, n)
+        pick(7)
+        magnitudes(1, [3])
+        quant_pass(1, nc.vector.tensor_copy)
+        for n in range(T2 // P):
+            second_product(1, n)
+            res = offset[n // 4][:, n % 4, :]
+            nc.vector.tensor_tensor(res, score[n][:], res, ADD)
+            nc.scalar.activation(res, res, ACT.Tanh)
+            nc.sync.dma_start(out[P * n : P * (n + 1), :], res)

@@ -56,22 +56,27 @@ def tile_list_bogie_benchmark_scores_kernel(
         idx1 = sb([P, S // 16], U16, "idx1")
         idx2 = sb([P, S // 16], U16, "idx2")
         idx3 = sb([P, NB // 16], U16, "idx3")
-        nc.sync.dma_start(idx1[:], offs)
-        for q in range(4):
-            nc.gpsimd.dma_start(
-                tab_sc[32 * q : 32 * q + 4, :, :].bitcast(I32),
-                tab_scales[:, 4 * q : 4 * q + 4, :].rearrange("a r t -> r a t").bitcast(I32),
-            )
-        for q in range(4):
-            nc.gpsimd.dma_start(
-                w4_sc_raw[32 * q : 32 * q + 4, :, :].bitcast(I32),
-                w4_scales[:, 4 * q : 4 * q + 4, :].rearrange("a r c -> r a c").bitcast(I32),
-            )
-        for v, vec in enumerate((gain, sq, gv)):
-            nc.gpsimd.dma_start(
-                rows[4 * v : 4 * v + 4, :].rearrange("t (n i) -> t n i", i=4),
-                vec.rearrange("(n t i) -> t n i", t=4, i=4),
-            )
+
+        def load_tab_scales():
+            for q in range(4):
+                nc.sync.dma_start(
+                    tab_sc[32 * q : 32 * q + 4, :, :].bitcast(I32),
+                    tab_scales[:, 4 * q : 4 * q + 4, :].rearrange("a r t -> r a t").bitcast(I32),
+                )
+
+        def load_w4_scales():
+            for q in range(4):
+                nc.sync.dma_start(
+                    w4_sc_raw[32 * q : 32 * q + 4, :, :].bitcast(I32),
+                    w4_scales[:, 4 * q : 4 * q + 4, :].rearrange("a r c -> r a c").bitcast(I32),
+                )
+
+        def load_rows():
+            for v, vec in enumerate((gain, sq, gv)):
+                nc.sync.dma_start(
+                    rows[4 * v : 4 * v + 4, :].rearrange("t (n i) -> t n i", i=4),
+                    vec.rearrange("(n t i) -> t n i", t=4, i=4),
+                )
 
         make_identity(nc, ident[:])
 
@@ -109,7 +114,7 @@ def tile_list_bogie_benchmark_scores_kernel(
         def load_wg(t):
             wg[t] = sb([P, S], F32, "wg%d" % t)
             for c in range(4):
-                (nc.gpsimd if t == 0 else nc.sync).dma_start(wg[t][32 * c : 32 * c + 32, :], wgs.rearrange("(n t i) j -> t n i j", t=4, i=4)[t])
+                nc.sync.dma_start(wg[t][32 * c : 32 * c + 32, :], wgs.rearrange("(n t i) j -> t n i j", t=4, i=4)[t])
 
         w1_in = {}
         w1_q = {}
@@ -141,9 +146,13 @@ def tile_list_bogie_benchmark_scores_kernel(
             )
 
         load_w1(0, 0)
+        load_tab_scales()
+        nc.sync.dma_start(idx1[:], offs)
         load_tab(0)
         load_w4(0)
+        load_w4_scales()
         load_w1(0, 1)
+        load_rows()
         load_tab(1)
         load_w1(0, 2)
         load_tab(2)
@@ -222,13 +231,13 @@ def tile_list_bogie_benchmark_scores_kernel(
         tanh_a(0)
 
         load_w1(1, 0)
+        load_w1(1, 1)
         load_w4(1)
+        load_w1(1, 2)
         load_page(2)
         load_wg(2)
-        load_w1(1, 1)
         load_page(3)
         load_wg(3)
-        load_w1(1, 2)
         for s in range(4, 8):
             load_page(s)
         deal_w4(1)
@@ -257,46 +266,80 @@ def tile_list_bogie_benchmark_scores_kernel(
         def place(s, h):
             b, t = divmod(s, PACK)
             nc.vector.tensor_tensor(page[s][:].indirect(idx2[:]), h[:], wg[t][:], MULT)
-            if t == 0:
-                pairs[b] = sb([P, 2, T2, 2], BF16, "pairs%d" % b, stage_tags[b])
-            nc.gpsimd.tensor_scalar(pairs[b][:, t // 2, :, t % 2], page[s][:], 1.0, 0.0, MULT, ADD)
+
+        def round_page(s, cols):
+            b, t = divmod(s, PACK)
+            if b not in pairs:
+                pairs[b] = sb([P, 2, T2, 2], BF16, "pairs%d" % b, stage_tags[2])
+            nc.scalar.copy(pairs[b][:, t // 2, cols, t % 2], page[s][:, cols])
 
         def pick(s):
             picked[s] = ring.tile([P, NB], F32, name="picked%d" % s, tag="picked")
             nc.vector.tensor_copy(picked[s][:], page[s][:].indirect(idx3[:]))
 
-        root = {}
         xpairs = {}
+        low, high = slice(0, T2 // 2), slice(T2 // 2, T2)
 
-        def magnitudes(b, ts):
-            if b not in root:
-                root[b] = sb([P, PACK, NB], F32, "root%d" % b, "root")
+        root = {}
+
+        def square(s):
+            if s % 2 == 0:
+                both = sb([P, 2, NB], F32, "root%d" % s, "root")
+                root[s], root[s + 1] = both[:, 0, :], both[:, 1, :]
+            if s == 7:
+                nc.vector.tensor_tensor(root[s], picked[s][:], picked[s][:], MULT)
+            else:
+                nc.scalar.activation(root[s], picked[s][:], ACT.Square)
+
+        def smooth(s):
+            nc.scalar.activation(root[s], root[s], ACT.Sqrt, bias=vec_col(1, s))
+
+        def weigh(s):
+            b, t = divmod(s, PACK)
+            if t == 0:
                 xpairs[b] = sb([P, 2, NB, 2], BF16, "xpairs%d" % b, "xpairs")
-            for t in ts:
-                nc.scalar.activation(root[b][:, t, :], picked[PACK * b + t][:], ACT.Square)
-            for t in ts:
-                nc.scalar.activation(root[b][:, t, :], root[b][:, t, :], ACT.Sqrt, bias=vec_col(1, PACK * b + t))
-            for t in ts:
-                nc.scalar.activation(
-                    xpairs[b][:, t // 2, :, t % 2], root[b][:, t, :], ACT.Copy, scale=vec_col(2, PACK * b + t)
-                )
+            nc.scalar.activation(xpairs[b][:, t // 2, :, t % 2], root[s], ACT.Copy, scale=vec_col(2, s))
+
+        def round_two(s):
+            for step in (lambda i: round_page(i, slice(0, T2)), square, smooth, weigh):
+                step(s)
+                step(s + 1)
+
+        def round_one(s):
+            square(s)
+            round_page(s, low)
+            smooth(s)
+            round_page(s, high)
+            weigh(s)
 
         p_q, p_s, x_q, x_s = {}, {}, {}, {}
 
-        def weave(copy, src, width, name, tag):
-            woven = sb([P, width, 2], F32, name, tag)
-            copy(woven[:], src[:].rearrange("p u c e -> p u (c e)").bitcast(F32).rearrange("p u c -> p c u"))
-            return woven[:].rearrange("p c u -> p (c u)").bitcast(BF16)
+        p_in, x_in = {}, {}
 
-        def quant_pass(b, copy):
-            p_in = weave(copy, pairs[b], T2, "p_in%d" % b, "pin%d" % b)
-            x_in = weave(copy, xpairs[b], NB, "x_in%d" % b, "xin%d" % b)
-            p_q[b] = sb([P, T2], U32, "p_q%d" % b)
-            p_s[b] = sb([P, T2], U8, "p_s%d" % b)
+        def weave_and_quantise(copy, src, woven, codes, scales, cols):
+            words = src[:].rearrange("p u c e -> p u (c e)").bitcast(F32)
+            copy(
+                woven[:, cols, :].rearrange("p (c i) u -> p c u i", i=4),
+                words[:, :, cols].rearrange("p u (c i) -> p c u i", i=4),
+            )
+            nc.vector.quantize_mx(
+                codes[:, cols].bitcast(FP8X4),
+                scales[:, cols],
+                woven[:, cols, :].rearrange("p c u -> p (c u)").bitcast(BF16),
+            )
+
+        def quant_page(b, copy, cols):
+            if b not in p_in:
+                p_in[b] = sb([P, T2, 2], F32, "p_in%d" % b, "pin%d" % b)
+                p_q[b] = sb([P, T2], U32, "p_q%d" % b)
+                p_s[b] = sb([P, T2], U8, "p_s%d" % b)
+            weave_and_quantise(copy, pairs[b], p_in[b], p_q[b], p_s[b], cols)
+
+        def quant_x(b, copy):
+            x_in[b] = sb([P, NB, 2], F32, "x_in%d" % b, "xin%d" % b)
             x_q[b] = sb([P, NB], U32, "x_q%d" % b)
             x_s[b] = sb([P, NB], U8, "x_s%d" % b)
-            nc.vector.quantize_mx(p_q[b][:].bitcast(FP8X4), p_s[b][:], p_in)
-            nc.vector.quantize_mx(x_q[b][:].bitcast(FP8X4), x_s[b][:], x_in)
+            weave_and_quantise(copy, xpairs[b], x_in[b], x_q[b], x_s[b], slice(0, NB))
 
         score = {}
 
@@ -323,11 +366,13 @@ def tile_list_bogie_benchmark_scores_kernel(
         h = features(4)
         pick(3)
         place(4, h)
-        magnitudes(0, range(PACK))
-        quant_pass(0, nc.scalar.copy)
+        round_two(0)
+        round_two(2)
+        quant_page(0, nc.scalar.copy, slice(0, T2))
+        quant_x(0, nc.scalar.copy)
 
         offset = {}
-        for half, tag in ((0, stage_tags[2]), (1, stage_tags[0])):
+        for half, tag in ((0, stage_tags[0]), (1, stage_tags[1])):
             offset[half] = sb([P, 4, NB], F32, "offset%d" % half, tag)
             nc.sync.dma_start(
                 offset[half][:], base[KP * half : KP * (half + 1), :].rearrange("(n p) j -> p n j", p=P)
@@ -337,12 +382,21 @@ def tile_list_bogie_benchmark_scores_kernel(
             h = features(s)
             pick(s - 1)
             place(s, h)
-            magnitudes(1, [s - 5])
+            if s == 6:
+                round_two(4)
+            if s == 7:
+                round_one(6)
         for n in range(T2 // P):
             second_product(0, n)
         pick(7)
-        magnitudes(1, [3])
-        quant_pass(1, nc.vector.tensor_copy)
+        square(7)
+        round_page(7, low)
+        round_page(7, high)
+        smooth(7)
+        weigh(7)
+        quant_page(1, nc.vector.tensor_copy, low)
+        quant_x(1, nc.vector.tensor_copy)
+        quant_page(1, nc.vector.tensor_copy, high)
         for n in range(T2 // P):
             second_product(1, n)
             res = offset[n // 4][:, n % 4, :]

@@ -42,14 +42,15 @@ def tile_list_bogie_benchmark_scores_kernel(
             return psum.tile([P, 512], F32, name=name, tag="bank%d" % i)
 
         tab_sc = sb([P, KA, T], U8, "tab_sc")
-        w4_sc_raw = sb([P, KA, H], U8, "w4_sc_raw", "xin1")
-        rows = sb([P, 2 * P], F32, "rows")
+        w4_sc_raw = {0: sb([P, KA, KP], U8, "w4_sc_raw0", "xin1"), 1: sb([P, KA, KP], U8, "w4_sc_raw1")}
+        rows = sb([3, H], F32, "rows")
+        rows_dealt = sb([P, H], F32, "rows_dealt", "xpairs")
         zero = sb([P, 1], F32, "zero")
         ident = sb([P, P], F32, "ident")
+        nc.gpsimd.memset(zero[:], 0.0)
         nc.vector.memset(tab_sc[:].rearrange("p a t -> p (a t)").bitcast(I32), 0)
-        nc.vector.memset(w4_sc_raw[:].rearrange("p a c -> p (a c)").bitcast(I32), 0)
-        nc.vector.memset(rows[:], 0.0)
-        nc.vector.memset(zero[:], 0.0)
+        for b in range(RB):
+            nc.vector.memset(w4_sc_raw[b][:].rearrange("p a c -> p (a c)").bitcast(I32), 0)
         zero_bias = sb([P, 1], F32, "zero_bias", "root")
         nc.scalar.activation(zero_bias[:], zero[:], ACT.Tanh)
 
@@ -58,27 +59,25 @@ def tile_list_bogie_benchmark_scores_kernel(
         idx3 = sb([P, NB // 16], U16, "idx3")
 
         def load_tab_scales():
-            for q in range(4):
+            for r in range(4):
                 nc.sync.dma_start(
-                    tab_sc[32 * q : 32 * q + 4, :, :].bitcast(I32),
-                    tab_scales[:, 4 * q : 4 * q + 4, :].rearrange("a r t -> r a t").bitcast(I32),
+                    tab_sc[r:P:32, :, :].bitcast(I32),
+                    tab_scales.rearrange("a (q r) t -> r q a t", r=4)[r].bitcast(I32),
                 )
 
-        def load_w4_scales():
-            for q in range(4):
+        def load_w4_scales(b):
+            for r in range(4):
                 nc.sync.dma_start(
-                    w4_sc_raw[32 * q : 32 * q + 4, :, :].bitcast(I32),
-                    w4_scales[:, 4 * q : 4 * q + 4, :].rearrange("a r c -> r a c").bitcast(I32),
+                    w4_sc_raw[b][r:P:32, :, :].bitcast(I32),
+                    w4_scales.rearrange("a (q r) c -> r q a c", r=4)[r][:, :, KP * b : KP * (b + 1)].bitcast(I32),
                 )
 
         def load_rows():
             for v, vec in enumerate((gain, sq, gv)):
-                nc.sync.dma_start(
-                    rows[4 * v : 4 * v + 4, :].rearrange("t (n i) -> t n i", i=4),
-                    vec.rearrange("(n t i) -> t n i", t=4, i=4),
-                )
+                nc.sync.dma_start(rows[v : v + 1, :], vec.rearrange("(o r) -> o r", o=1))
 
         make_identity(nc, ident[:])
+        nc.gpsimd.memset(rows_dealt[:], 0.0)
 
         stage_tags = ["stage0", "stage1", "stage2"]
         w1_raw = {}
@@ -137,6 +136,7 @@ def tile_list_bogie_benchmark_scores_kernel(
             nc.vector.quantize_mx(w1_q[b, a][:].bitcast(FP8X4), w1_s[b, a][:], w1_in[b, a][:])
 
         w4_q = {}
+        w4_s = {}
 
         def deal_w4(b):
             w4_q[b] = sb([P, KA, 2 * KP], U8, "w4_q%d" % b)
@@ -144,16 +144,21 @@ def tile_list_bogie_benchmark_scores_kernel(
                 w4_q[b][:].bitcast(I32).rearrange("p a (t n w) -> p a t n w", t=4, w=2),
                 w4_raw[b][:].bitcast(I32).rearrange("p a (n t w) -> p a t n w", t=4, w=2),
             )
+            w4_s[b] = sb([P, KA, KP], U8, "w4_s%d" % b)
+            nc.vector.tensor_copy(
+                w4_s[b][:].bitcast(I32).rearrange("p a (t n) -> p a t n", t=4),
+                w4_sc_raw[b][:].bitcast(I32).rearrange("p a (n t) -> p a t n", t=4),
+            )
 
         load_w1(0, 0)
         load_tab_scales()
-        nc.sync.dma_start(idx1[:], offs)
         load_tab(0)
-        load_w4(0)
-        load_w4_scales()
         load_w1(0, 1)
+        nc.sync.dma_start(idx1[:], offs)
         load_rows()
         load_tab(1)
+        load_w4(0)
+        load_w4_scales(0)
         load_w1(0, 2)
         load_tab(2)
         nc.sync.dma_start(idx2[:], offs2)
@@ -163,31 +168,32 @@ def tile_list_bogie_benchmark_scores_kernel(
         load_page(1)
         load_wg(1)
 
-        vecs = sb([P, RB, 12], F32, "vecs")
-        turned = bank(7, "turned")
+        vecs = sb([P, RB, PACK, 3], F32, "vecs")
+        nc.scalar.copy(
+            rows_dealt[0:3, :].rearrange("v (b t n i) -> v b t n i", b=RB, t=4, i=4),
+            rows[:].rearrange("v (b n t i) -> v b t n i", b=RB, t=4, i=4),
+        )
         for b in range(RB):
-            nc.tensor.transpose(turned[:, P * b : P * (b + 1)], rows[:, P * b : P * (b + 1)], ident[:])
-        nc.scalar.copy(vecs[:], turned[:, 0 : 2 * P].rearrange("p (b c) -> p b c", b=RB)[:, :, 0:12])
+            turned = bank(6 + b, "turned%d" % b)
+            for t in range(PACK):
+                c0 = KP * b + P * t
+                nc.tensor.transpose(turned[:, P * t : P * (t + 1)], rows_dealt[:, c0 : c0 + P], ident[:])
+            nc.scalar.copy(vecs[:, b], turned[:].rearrange("p (t c) -> p t c", t=PACK)[:, :, 0:3])
 
         def vec_col(v, s):
             b, t = divmod(s, PACK)
-            return vecs[:, b, 4 * v + t : 4 * v + t + 1]
+            return vecs[:, b, t, v : v + 1]
 
         v_s = sb([P, KA, S], U8, "v_s")
         for a in range(KA):
             nc.vector.tensor_copy(v_s[:, a, :], tab_sc[:, a, :].indirect(idx1[:]))
-        w4_s = sb([P, KA, H], U8, "w4_s")
-        nc.vector.tensor_copy(
-            w4_s[:].bitcast(I32).rearrange("p a (b t n) -> p a b t n", b=RB, t=4),
-            w4_sc_raw[:].bitcast(I32).rearrange("p a (b n t) -> p a b t n", b=RB, t=4),
-        )
         v_q = {}
         for a in range(KA):
             cast_w1(0, a, a == KA - 1)
             quant_w1(0, a)
             v_q[a] = sb([P, S], U32, "v_q%d" % a)
             nc.vector.tensor_copy(v_q[a][:], tab[a][:].indirect(idx1[:]))
-            if a == 0:
+            if a == 1:
                 deal_w4(0)
 
         acc_a = {}
@@ -212,7 +218,7 @@ def tile_list_bogie_benchmark_scores_kernel(
                     nc.tensor.matmul_mx(
                         acc_b[s][:],
                         lhsT=w4_q[b][:, a, 2 * P * t : 2 * P * (t + 1)].bitcast(FP4X4),
-                        lhsT_scale=w4_s[:, a, KP * b + P * t : KP * b + P * (t + 1)],
+                        lhsT_scale=w4_s[b][:, a, P * t : P * (t + 1)],
                         rhs=v_q[a][:].bitcast(FP8X4),
                         rhs_scale=v_s[:, a, :],
                         start=(a == 0),
@@ -233,6 +239,7 @@ def tile_list_bogie_benchmark_scores_kernel(
         load_w1(1, 0)
         load_w1(1, 1)
         load_w4(1)
+        load_w4_scales(1)
         load_w1(1, 2)
         load_page(2)
         load_wg(2)

@@ -150,11 +150,11 @@ def tile_list_bogie_benchmark_scores_kernel(
                 w4_sc_raw[b][:].bitcast(I32).rearrange("p a (n t) -> p a t n", t=4),
             )
 
+        nc.sync.dma_start(idx1[:], offs)
         load_w1(0, 0)
         load_tab_scales()
         load_tab(0)
         load_w1(0, 1)
-        nc.sync.dma_start(idx1[:], offs)
         load_rows()
         load_tab(1)
         load_w4(0)
@@ -162,23 +162,24 @@ def tile_list_bogie_benchmark_scores_kernel(
         load_w1(0, 2)
         load_tab(2)
         nc.sync.dma_start(idx2[:], offs2)
-        load_wg(0)
         load_page(0)
-        nc.sync.dma_start(idx3[:], offs3)
+        load_wg(0)
         load_page(1)
-        load_wg(1)
+        nc.sync.dma_start(idx3[:], offs3)
 
         vecs = sb([P, RB, PACK, 3], F32, "vecs")
-        nc.scalar.copy(
-            rows_dealt[0:3, :].rearrange("v (b t n i) -> v b t n i", b=RB, t=4, i=4),
-            rows[:].rearrange("v (b n t i) -> v b t n i", b=RB, t=4, i=4),
-        )
-        for b in range(RB):
-            turned = bank(6 + b, "turned%d" % b)
-            for t in range(PACK):
-                c0 = KP * b + P * t
-                nc.tensor.transpose(turned[:, P * t : P * (t + 1)], rows_dealt[:, c0 : c0 + P], ident[:])
-            nc.scalar.copy(vecs[:, b], turned[:].rearrange("p (t c) -> p t c", t=PACK)[:, :, 0:3])
+
+        def turn_rows():
+            nc.scalar.copy(
+                rows_dealt[0:3, :].rearrange("v (b t n i) -> v b t n i", b=RB, t=4, i=4),
+                rows[:].rearrange("v (b n t i) -> v b t n i", b=RB, t=4, i=4),
+            )
+            for b in range(RB):
+                turned = bank(6 + b, "turned%d" % b)
+                for t in range(PACK):
+                    c0 = KP * b + P * t
+                    nc.tensor.transpose(turned[:, P * t : P * (t + 1)], rows_dealt[:, c0 : c0 + P], ident[:])
+                nc.scalar.copy(vecs[:, b], turned[:].rearrange("p (t c) -> p t c", t=PACK)[:, :, 0:3])
 
         def vec_col(v, s):
             b, t = divmod(s, PACK)
@@ -199,12 +200,12 @@ def tile_list_bogie_benchmark_scores_kernel(
         acc_a = {}
         acc_b = {}
 
-        def first_products(b):
-            for t in range(PACK):
+        def first_products(b, ts):
+            for t in ts:
                 acc_a[PACK * b + t] = bank(2 * t, "acc_a%d%d" % (b, t))
                 acc_b[PACK * b + t] = bank(2 * t + 1, "acc_b%d%d" % (b, t))
             for a in range(KA):
-                for t in range(PACK):
+                for t in ts:
                     s = PACK * b + t
                     nc.tensor.matmul_mx(
                         acc_a[s][:],
@@ -233,10 +234,13 @@ def tile_list_bogie_benchmark_scores_kernel(
                 th[s] = ring.tile([P, S], F32, name="th%d" % s, tag="th")
                 nc.scalar.activation(th[s][:], acc_a[s][:], ACT.Tanh, bias=zero_bias[:])
 
-        first_products(0)
+        first_products(0, range(PACK - 1))
+        turn_rows()
+        first_products(0, [PACK - 1])
         tanh_a(0)
 
         load_w1(1, 0)
+        load_wg(1)
         load_w1(1, 1)
         load_w4(1)
         load_w4_scales(1)
@@ -254,8 +258,8 @@ def tile_list_bogie_benchmark_scores_kernel(
 
         picked = {}
         pairs = {}
-        held_u = {7: "pin0"}
-        held_h = {3: "held", 7: "xin0"}
+        held_u = {2: "pin1", 7: "pin0"}
+        held_h = {2: "w1_in1", 3: "held", 7: "xin0"}
 
         def features(s):
             if s in held_u:
@@ -368,7 +372,7 @@ def tile_list_bogie_benchmark_scores_kernel(
             if s > 0:
                 pick(s - 1)
             place(s, h)
-        first_products(1)
+        first_products(1, range(PACK))
         tanh_a(1)
         h = features(4)
         pick(3)

from contextlib import ExitStack

import concourse.mybir as mybir
from concourse.masks import make_identity

K, H, T, S, T2, NB = 1536, 1024, 2048, 512, 1024, 512
FLOPS = 2 * (2 * K * H * S + H * T2 * NB)

F32 = mybir.dt.float32
BF16 = mybir.dt.bfloat16
I32 = mybir.dt.int32
U32 = mybir.dt.uint32
U16 = mybir.dt.uint16
U8 = mybir.dt.uint8
FP8X4 = mybir.dt.float8_e4m3fn_x4
FP4X4 = mybir.dt.float4_e2m1fn_x4
MULT = mybir.AluOpType.mult
ADD = mybir.AluOpType.add
ACT = mybir.ActivationFunctionType

P = 128
PACK = 4
KP = P * PACK
KA = K // KP
RB = H // KP
AL = 64


def tile_list_bogie_benchmark_scores_kernel(
    tc, tab_words, tab_scales, offs, offs2, offs3, w1, w4_words, w4_scales, gain, wgs, page0, sq, gv, base, out
):
    nc = tc.nc
    with ExitStack() as ctx:
        keep = ctx.enter_context(tc.tile_pool(name="keep", bufs=1))
        ring = ctx.enter_context(tc.tile_pool(name="ring", bufs=4))
        psum = ctx.enter_context(tc.psum_pool(name="psum", bufs=1))

        def sb(shape, dtype, name, tag=None):
            return keep.tile(shape, dtype, name=name, tag=tag or name, align_bytes=AL)

        def bank(i, name):
            return psum.tile([P, 512], F32, name=name, tag="bank%d" % i)

        tab_sc = sb([P, KA, T], U8, "tab_sc")
        w4_sc_raw = {0: sb([P, KA, KP], U8, "w4_sc_raw0", "xin1"), 1: sb([P, KA, KP], U8, "w4_sc_raw1")}
        rows = sb([3, H], F32, "rows")
        rows_dealt = sb([P, H], F32, "rows_dealt", "xpairs")
        zero = sb([P, 1], F32, "zero")
        ident = sb([P, P], F32, "ident")
        nc.gpsimd.memset(zero[:], 0.0)
        nc.vector.memset(tab_sc[:].rearrange("p a t -> p (a t)").bitcast(I32), 0)
        for b in range(RB):
            nc.vector.memset(w4_sc_raw[b][:].rearrange("p a c -> p (a c)").bitcast(I32), 0)
        zero_bias = sb([P, 1], F32, "zero_bias", "root")
        nc.scalar.activation(zero_bias[:], zero[:], ACT.Tanh)

        idx1 = sb([P, S // 16], U16, "idx1")
        idx2 = sb([P, S // 16], U16, "idx2")
        idx3 = sb([P, NB // 16], U16, "idx3")

        def load_tab_scales():
            for r in range(4):
                nc.sync.dma_start(
                    tab_sc[r:P:32, :, :].bitcast(I32),
                    tab_scales.rearrange("a (q r) t -> r q a t", r=4)[r].bitcast(I32),
                )

        def load_w4_scales(b):
            for r in range(4):
                nc.sync.dma_start(
                    w4_sc_raw[b][r:P:32, :, :].bitcast(I32),
                    w4_scales.rearrange("a (q r) c -> r q a c", r=4)[r][:, :, KP * b : KP * (b + 1)].bitcast(I32),
                )

        def load_rows():
            for v, vec in enumerate((gain, sq, gv)):
                nc.sync.dma_start(rows[v : v + 1, :], vec.rearrange("(o r) -> o r", o=1))

        make_identity(nc, ident[:])
        nc.gpsimd.memset(rows_dealt[:], 0.0)

        stage_tags = ["stage0", "stage1", "stage2"]
        w1_raw = {}
        tab = {}
        w4_raw = {}
        page = {}
        wg = {}

        def load_w1(b, a):
            w1_raw[b, a] = sb([P, PACK, KP], F32, "w1_raw%d%d" % (b, a), stage_tags[a])
            nc.sync.dma_start(
                w1_raw[b, a][:], w1[KP * a : KP * (a + 1), KP * b : KP * (b + 1)].rearrange("(p j) c -> p j c", j=PACK)
            )

        def load_tab(a):
            tab[a] = sb([P, T], U32, "tab%d" % a)
            nc.sync.dma_start(tab[a][:].bitcast(I32), tab_words[a].rearrange("p t i -> p (t i)").bitcast(I32))

        def load_w4(b):
            w4_raw[b] = sb([P, KA, 2 * KP], U8, "w4_raw%d" % b, "pin1" if b == 1 else None)
            nc.sync.dma_start(
                w4_raw[b][:].bitcast(I32),
                w4_words.rearrange("a p c -> p a c")[:, :, 2 * KP * b : 2 * KP * (b + 1)].bitcast(I32),
            )

        def load_page(s):
            b, t = divmod(s, PACK)
            page[s] = sb([P, T2], F32, "page%d" % s)
            nc.sync.dma_start(
                page[s][:], page0[KP * b : KP * (b + 1), :].rearrange("(n t i) m -> t n i m", t=4, i=4)[t]
            )

        def load_wg(t):
            wg[t] = sb([P, S], F32, "wg%d" % t)
            for c in range(4):
                nc.sync.dma_start(wg[t][32 * c : 32 * c + 32, :], wgs.rearrange("(n t i) j -> t n i j", t=4, i=4)[t])

        w1_in = {}
        w1_q = {}
        w1_s = {}

        def cast_w1(b, a, split):
            tag = "held" if (b, a) == (1, 2) else "w1_in%d" % (a % 2)
            w1_in[b, a] = sb([P, PACK * KP], BF16, "w1_in%d%d" % (b, a), tag)
            dst = w1_in[b, a][:].rearrange("p (t n i j) -> p t n j i", t=4, i=4, j=4)
            src = w1_raw[b, a][:].rearrange("p j (n t i) -> p t n j i", t=4, i=4)
            if split:
                nc.vector.tensor_copy(dst[:, 0:2], src[:, 0:2])
                nc.scalar.copy(dst[:, 2:4], src[:, 2:4])
            else:
                nc.scalar.copy(dst, src)

        def quant_w1(b, a):
            w1_q[b, a] = sb([P, KP], U32, "w1_q%d%d" % (b, a))
            w1_s[b, a] = sb([P, KP], U8, "w1_s%d%d" % (b, a))
            nc.vector.quantize_mx(w1_q[b, a][:].bitcast(FP8X4), w1_s[b, a][:], w1_in[b, a][:])

        w4_q = {}
        w4_s = {}

        def deal_w4(b):
            w4_q[b] = sb([P, KA, 2 * KP], U8, "w4_q%d" % b)
            nc.vector.tensor_copy(
                w4_q[b][:].bitcast(I32).rearrange("p a (t n w) -> p a t n w", t=4, w=2),
                w4_raw[b][:].bitcast(I32).rearrange("p a (n t w) -> p a t n w", t=4, w=2),
            )
            w4_s[b] = sb([P, KA, KP], U8, "w4_s%d" % b)
            nc.vector.tensor_copy(
                w4_s[b][:].bitcast(I32).rearrange("p a (t n) -> p a t n", t=4),
                w4_sc_raw[b][:].bitcast(I32).rearrange("p a (n t) -> p a t n", t=4),
            )

        nc.sync.dma_start(idx1[:], offs)
        load_w1(0, 0)
        load_tab_scales()
        load_tab(0)
        load_w1(0, 1)
        load_rows()
        load_tab(1)
        load_w4(0)
        load_w4_scales(0)
        load_w1(0, 2)
        load_tab(2)
        nc.sync.dma_start(idx2[:], offs2)
        load_page(0)
        load_wg(0)
        load_page(1)
        nc.sync.dma_start(idx3[:], offs3)

        vecs = sb([P, RB, PACK, 3], F32, "vecs")

        def turn_rows():
            nc.scalar.copy(
                rows_dealt[0:3, :].rearrange("v (b t n i) -> v b t n i", b=RB, t=4, i=4),
                rows[:].rearrange("v (b n t i) -> v b t n i", b=RB, t=4, i=4),
            )
            for b in range(RB):
                turned = bank(6 + b, "turned%d" % b)
                for t in range(PACK):
                    c0 = KP * b + P * t
                    nc.tensor.transpose(turned[:, P * t : P * (t + 1)], rows_dealt[:, c0 : c0 + P], ident[:])
                nc.scalar.copy(vecs[:, b], turned[:].rearrange("p (t c) -> p t c", t=PACK)[:, :, 0:3])

        def vec_col(v, s):
            b, t = divmod(s, PACK)
            return vecs[:, b, t, v : v + 1]

        v_s = sb([P, KA, S], U8, "v_s")
        for a in range(KA):
            nc.vector.tensor_copy(v_s[:, a, :], tab_sc[:, a, :].indirect(idx1[:]))
        v_q = {}
        for a in range(KA):
            cast_w1(0, a, a == KA - 1)
            quant_w1(0, a)
            v_q[a] = sb([P, S], U32, "v_q%d" % a)
            nc.vector.tensor_copy(v_q[a][:], tab[a][:].indirect(idx1[:]))
            if a == 1:
                deal_w4(0)

        acc_a = {}
        acc_b = {}

        def first_products(b, ts):
            for t in ts:
                acc_a[PACK * b + t] = bank(2 * t, "acc_a%d%d" % (b, t))
                acc_b[PACK * b + t] = bank(2 * t + 1, "acc_b%d%d" % (b, t))
            for a in range(KA):
                for t in ts:
                    s = PACK * b + t
                    nc.tensor.matmul_mx(
                        acc_a[s][:],
                        lhsT=w1_q[b, a][:, P * t : P * (t + 1)].bitcast(FP8X4),
                        lhsT_scale=w1_s[b, a][:, P * t : P * (t + 1)],
                        rhs=v_q[a][:].bitcast(FP8X4),
                        rhs_scale=v_s[:, a, :],
                        start=(a == 0),
                        stop=(a == KA - 1),
                    )
                    nc.tensor.matmul_mx(
                        acc_b[s][:],
                        lhsT=w4_q[b][:, a, 2 * P * t : 2 * P * (t + 1)].bitcast(FP4X4),
                        lhsT_scale=w4_s[b][:, a, P * t : P * (t + 1)],
                        rhs=v_q[a][:].bitcast(FP8X4),
                        rhs_scale=v_s[:, a, :],
                        start=(a == 0),
                        stop=(a == KA - 1),
                    )

        th = {}

        def tanh_a(b):
            for t in range(PACK):
                s = PACK * b + t
                th[s] = ring.tile([P, S], F32, name="th%d" % s, tag="th")
                nc.scalar.activation(th[s][:], acc_a[s][:], ACT.Tanh, bias=zero_bias[:])

        first_products(0, range(PACK - 1))
        turn_rows()
        first_products(0, [PACK - 1])
        tanh_a(0)

        load_w1(1, 0)
        load_wg(1)
        load_w1(1, 1)
        load_w4(1)
        load_w4_scales(1)
        load_w1(1, 2)
        load_page(2)
        load_wg(2)
        load_page(3)
        load_wg(3)
        for s in range(4, 8):
            load_page(s)
        deal_w4(1)
        for a in range(KA):
            cast_w1(1, a, False)
            quant_w1(1, a)

        picked = {}
        pairs = {}
        held_u = {2: "pin1", 7: "pin0"}
        held_h = {2: "w1_in1", 3: "held", 7: "xin0"}

        def features(s):
            if s in held_u:
                u = sb([P, S], F32, "u%d" % s, held_u[s])
            else:
                u = ring.tile([P, S], F32, name="u%d" % s, tag="u", bufs=2)
            if s in held_h:
                h = sb([P, S], F32, "h%d" % s, held_h[s])
            else:
                h = ring.tile([P, S], F32, name="h%d" % s, tag="h", bufs=3)
            nc.vector.scalar_tensor_tensor(u[:], acc_b[s][:], vec_col(0, s), th[s][:], MULT, MULT)
            nc.vector.scalar_tensor_tensor(h[:], acc_a[s][:], vec_col(0, s), u[:], MULT, ADD)
            return h

        def place(s, h):
            b, t = divmod(s, PACK)
            nc.vector.tensor_tensor(page[s][:].indirect(idx2[:]), h[:], wg[t][:], MULT)

        def round_page(s, cols):
            b, t = divmod(s, PACK)
            if b not in pairs:
                pairs[b] = sb([P, 2, T2, 2], BF16, "pairs%d" % b, stage_tags[2])
            nc.scalar.copy(pairs[b][:, t // 2, cols, t % 2], page[s][:, cols])

        def pick(s):
            picked[s] = ring.tile([P, NB], F32, name="picked%d" % s, tag="picked")
            nc.vector.tensor_copy(picked[s][:], page[s][:].indirect(idx3[:]))

        xpairs = {}
        low, high = slice(0, T2 // 2), slice(T2 // 2, T2)

        root = {}

        def square(s):
            if s % 2 == 0:
                both = sb([P, 2, NB], F32, "root%d" % s, "root")
                root[s], root[s + 1] = both[:, 0, :], both[:, 1, :]
            if s == 7:
                nc.vector.tensor_tensor(root[s], picked[s][:], picked[s][:], MULT)
            else:
                nc.scalar.activation(root[s], picked[s][:], ACT.Square)

        def smooth(s):
            nc.scalar.activation(root[s], root[s], ACT.Sqrt, bias=vec_col(1, s))

        def weigh(s):
            b, t = divmod(s, PACK)
            if t == 0:
                xpairs[b] = sb([P, 2, NB, 2], BF16, "xpairs%d" % b, "xpairs")
            nc.scalar.activation(xpairs[b][:, t // 2, :, t % 2], root[s], ACT.Copy, scale=vec_col(2, s))

        def round_two(s):
            for step in (lambda i: round_page(i, slice(0, T2)), square, smooth, weigh):
                step(s)
                step(s + 1)

        def round_one(s):
            square(s)
            round_page(s, low)
            smooth(s)
            round_page(s, high)
            weigh(s)

        p_q, p_s, x_q, x_s = {}, {}, {}, {}

        p_in, x_in = {}, {}

        def weave_and_quantise(copy, src, woven, codes, scales, cols):
            words = src[:].rearrange("p u c e -> p u (c e)").bitcast(F32)
            copy(
                woven[:, cols, :].rearrange("p (c i) u -> p c u i", i=4),
                words[:, :, cols].rearrange("p u (c i) -> p c u i", i=4),
            )
            nc.vector.quantize_mx(
                codes[:, cols].bitcast(FP8X4),
                scales[:, cols],
                woven[:, cols, :].rearrange("p c u -> p (c u)").bitcast(BF16),
            )

        def quant_page(b, copy, cols):
            if b not in p_in:
                p_in[b] = sb([P, T2, 2], F32, "p_in%d" % b, "pin%d" % b)
                p_q[b] = sb([P, T2], U32, "p_q%d" % b)
                p_s[b] = sb([P, T2], U8, "p_s%d" % b)
            weave_and_quantise(copy, pairs[b], p_in[b], p_q[b], p_s[b], cols)

        def quant_x(b, copy):
            x_in[b] = sb([P, NB, 2], F32, "x_in%d" % b, "xin%d" % b)
            x_q[b] = sb([P, NB], U32, "x_q%d" % b)
            x_s[b] = sb([P, NB], U8, "x_s%d" % b)
            weave_and_quantise(copy, xpairs[b], x_in[b], x_q[b], x_s[b], slice(0, NB))

        score = {}

        def second_product(b, n):
            if b == 0:
                score[n] = bank(n, "score%d" % n)
            nc.tensor.matmul_mx(
                score[n][:],
                lhsT=p_q[b][:, P * n : P * (n + 1)].bitcast(FP8X4),
                lhsT_scale=p_s[b][:, P * n : P * (n + 1)],
                rhs=x_q[b][:].bitcast(FP8X4),
                rhs_scale=x_s[b][:],
                start=(b == 0),
                stop=(b == RB - 1),
            )

        for s in range(0, 4):
            h = features(s)
            if s > 0:
                pick(s - 1)
            place(s, h)
        first_products(1, range(PACK))
        tanh_a(1)
        h = features(4)
        pick(3)
        place(4, h)
        round_two(0)
        round_two(2)
        quant_page(0, nc.scalar.copy, slice(0, T2))
        quant_x(0, nc.scalar.copy)

        offset = {}
        for half, tag in ((0, stage_tags[0]), (1, stage_tags[1])):
            offset[half] = sb([P, 4, NB], F32, "offset%d" % half, tag)
            nc.sync.dma_start(
                offset[half][:], base[KP * half : KP * (half + 1), :].rearrange("(n p) j -> p n j", p=P)
            )

        for s in range(5, 8):
            h = features(s)
            pick(s - 1)
            place(s, h)
            if s == 6:
                round_two(4)
            if s == 7:
                round_one(6)
        for n in range(T2 // P):
            second_product(0, n)
        pick(7)
        square(7)
        round_page(7, low)
        round_page(7, high)
        smooth(7)
        weigh(7)
        quant_page(1, nc.vector.tensor_copy, low)
        quant_x(1, nc.vector.tensor_copy)
        quant_page(1, nc.vector.tensor_copy, high)
        for n in range(T2 // P):
            second_product(1, n)
            res = offset[n // 4][:, n % 4, :]
            nc.vector.tensor_tensor(res, score[n][:], res, ADD)
            nc.scalar.activation(res, res, ACT.Tanh)
            nc.sync.dma_start(out[P * n : P * (n + 1), :], res)
